import numpy as np
import ml_dtypes


def mxq(x, axis, fmt="e4m3"):
    dtype, down = {"e4m3": (ml_dtypes.float8_e4m3fn, 7), "e5m2": (ml_dtypes.float8_e5m2, 14)}[fmt]
    v = np.moveaxis(np.asarray(x, np.float32).astype(ml_dtypes.bfloat16).astype(np.float64), axis, -1)
    blocks = v.reshape(v.shape[:-1] + (-1, 32))
    amax = np.abs(blocks).max(-1, keepdims=True)
    byte = np.maximum(np.where(amax > 0, np.frexp(amax)[1] - 1 + 127, 0) - down, 1)
    scale = np.exp2(byte - 127.0)
    codes = (blocks / scale).astype(np.float32).astype(dtype).astype(np.float64)
    return np.moveaxis((codes * scale).reshape(v.shape), -1, axis)


WIDE = False


def mx_kscale(k):
    if not WIDE:
        return np.ones(k)
    levels = np.array([10, -10, 5, -5, 0])
    if k % 512:
        return np.exp2(np.random.permutation(np.resize(levels, k // 32))).repeat(32)
    a = np.empty((k // 512, 16))
    for p in range(k // 512):
        a[p, :8] = np.random.permutation(np.resize(levels, 8))
        for g in range(8):
            far = levels[np.abs(levels - a[p, g]) >= 10]
            a[p, g + 8] = far[np.random.randint(len(far))]
    return np.exp2(a.ravel()).repeat(32)


BF16 = ml_dtypes.bfloat16


def bf(x):
    return np.asarray(x, np.float32).astype(BF16)


def f64(x):
    return np.asarray(x).astype(np.float64)


E2M1 = np.array([0.0, 0.5, 1.0, 1.5, 2.0, 3.0, 4.0, 6.0, -0.0, -0.5, -1.0, -1.5, -2.0, -3.0, -4.0, -6.0])


def pack_weight(w, fmt):
    k, n = w.shape
    w = f64(bf(w)).reshape(k // 32, 32, n)
    amax = np.abs(w).max(1)
    if fmt == "e4m3":
        byte = np.frexp(amax)[1] - 1 + 127 - 7
    else:
        mant, ex = np.frexp(amax / 6.0)
        byte = np.where(mant > 0.5, ex, ex - 1) + 127
    byte = np.clip(np.where(amax > 0, byte, 1), 1, 254)
    scaled = (w * np.exp2(127.0 - byte)[:, None, :]).reshape(k, n).astype(np.float32)
    by_word = np.ascontiguousarray(scaled.reshape(k // 512, 128, 4, n).transpose(0, 1, 3, 2))
    if fmt == "e4m3":
        words = by_word.astype(ml_dtypes.float8_e4m3fn).view(np.uint8)
    else:
        c = by_word.astype(ml_dtypes.float4_e2m1fn).view(np.uint8) & 0xF
        words = c[..., 0::2] | (c[..., 1::2] << 4)
    return np.ascontiguousarray(words), np.ascontiguousarray(byte.astype(np.uint8).reshape(k // 512, 16, n))


def unpack_weight(words, scales, fmt):
    g, p, n, _ = words.shape
    if fmt == "e4m3":
        vals = np.ascontiguousarray(words).view(ml_dtypes.float8_e4m3fn).astype(np.float64)
    else:
        nib = np.empty((g, p, n, 4), np.uint8)
        nib[..., 0::2] = words & 0xF
        nib[..., 1::2] = words >> 4
        vals = E2M1[nib]
    vals = vals * np.repeat(np.exp2(scales.astype(np.float64) - 127.0), 8, axis=1)[..., None]
    return vals.transpose(0, 1, 3, 2).reshape(g * 512, n)
def pack4(w):
    words, scales = pack_weight(w, "e2m1")
    return words.reshape(words.shape[0], 128, -1), scales


def unpack4(words, scales):
    return unpack_weight(words.reshape(words.shape[0], 128, -1, 2), scales, "e2m1")


def planes(Y):
    n, m = Y.shape
    b = f64(bf(Y)).reshape(n // 32, 32, m)
    amax = np.abs(b).max(1)
    byte = np.clip(np.where(amax > 0, np.frexp(amax)[1] - 1 + 127 - 7, 1), 1, 254)
    codes = (b * np.exp2(127.0 - byte)[:, None, :]).reshape(n, m).astype(np.float32).astype(ml_dtypes.float8_e4m3fn).view(np.uint8)
    words = codes.reshape(n // 512, 128, 4, m).transpose(0, 1, 3, 2)
    return np.ascontiguousarray(words), np.ascontiguousarray(byte.astype(np.uint8).reshape(n // 512, 16, m))


C, K, F, M = 1536, 1024, 2048, 512


def setup_inputs():
    s = mx_kscale(K)
    t = mx_kscale(F)
    P = np.random.randn(K, C)
    T = np.random.randn(K, F) / np.sqrt(K)
    cost = 0.5 * np.random.randn(F)
    shifts = np.random.randn(F, M) / np.sqrt(F)
    duals_words, duals_scales = pack4(P / s[:, None])
    tech_words, tech_scales = pack4(T * s[:, None] * t[None, :])
    return {
        "duals_words": duals_words, "duals_scales": duals_scales,
        "tech_words": tech_words, "tech_scales": tech_scales,
        "cost": bf(cost * t),
        "shifts": bf(shifts / t[:, None]),
        "alpha": bf(0.5 * np.random.randn(C)),
        "weight": bf(np.exp(0.8 * np.random.randn(C))),
    }


def reference(duals_words, duals_scales, tech_words, tech_scales, cost, shifts, alpha, weight):
    P = unpack4(duals_words, duals_scales)
    T = unpack4(tech_words, tech_scales)
    D = f64(cost)[None, :] - (P.T @ T)
    v = mxq(D, 1) @ mxq(f64(shifts), 0)
    y = f64(weight)[:, None] * (v + f64(alpha)[:, None])
    Y = y.reshape(C, M)
    words, scales = planes(Y)
    return y, words, scales

@@ -1,0 +1,324 @@
+from contextlib import ExitStack
+
+import concourse.mybir as mybir
+from concourse.masks import make_identity
+
+C, K, F, M = 1536, 1024, 2048, 512
+FLOPS = 2 * K * C * F + 2 * C * F * M
+
+F32 = mybir.dt.float32
+BF16 = mybir.dt.bfloat16
+I32 = mybir.dt.int32
+U32 = mybir.dt.uint32
+U8 = mybir.dt.uint8
+FP8X4 = mybir.dt.float8_e4m3fn_x4
+FP4X4 = mybir.dt.float4_e2m1fn_x4
+IDENT = mybir.ActivationFunctionType.Identity
+MULT = mybir.AluOpType.mult
+ADD = mybir.AluOpType.add
+
+P = 128
+G = 512
+KP = K // G
+FG = F // G
+CG = C // G
+
+
+def tile_benders_cut_values_k5_kernel(
+    tc, duals_words, duals_scales, tech_words, tech_scales, cost, shifts, alpha, weight, out_0, out_1, out_2
+):
+    nc = tc.nc
+    with ExitStack() as ctx:
+        keep = ctx.enter_context(tc.tile_pool(name="keep", bufs=1))
+        stage = ctx.enter_context(tc.tile_pool(name="stage", bufs=3))
+        psum = ctx.enter_context(tc.psum_pool(name="psum", bufs=8))
+        ctx.enter_context(tc.manual_schedule())
+
+        def sb(name, shape, dtype):
+            return keep.tile(shape, dtype, name=name, align_bytes=256)
+
+        t_raw_first = sb("t_raw_first", [P, KP, 2 * G], U8)
+        t_raw_rest = sb("t_raw_rest", [P, KP, 2 * (F - G)], U8)
+        ts_raw_first = sb("ts_raw_first", [P, KP, G], U8)
+        ts_raw_rest = sb("ts_raw_rest", [P, KP, F - G], U8)
+        t_words = [sb("t_words%d" % g, [P, KP, 2 * G], U8) for g in range(FG)]
+        t_scales = [sb("t_scales%d" % g, [P, KP, G], U8) for g in range(FG)]
+        p_words = [sb("p_words%d" % c, [P, KP, 2 * G], U8) for c in range(CG)]
+        ps_first = sb("ps_first", [P, KP, 2 * G], U8)
+        ps_last = sb("ps_last", [P, KP, G], U8)
+        s_raw = [sb("s_raw%d" % g, [P, 4, M], BF16) for g in range(FG)]
+        s_codes = [sb("s_codes%d" % g, [P, M], U32) for g in range(FG)]
+        s_scales = [sb("s_scales%d" % g, [P, M], U8) for g in range(FG)]
+        d_rows = {(c, g): sb("d_rows%d_%d" % (c, g), [P, 4, G], BF16) for c in range(CG) for g in range(FG)}
+        d_codes = {(c, g): sb("d_codes%d_%d" % (c, g), [P, G], U32) for c in range(CG) for g in range(FG)}
+        d_scales = {(c, g): sb("d_scales%d_%d" % (c, g), [P, G], U8) for c in range(CG) for g in range(FG)}
+        cost_row = sb("cost_row", [FG, G], BF16)
+        cost_sorted = sb("cost_sorted", [P, 4, P], BF16)
+        cost_col = sb("cost_col", [P, 4, FG], F32)
+        ident = sb("ident", [P, P], BF16)
+        alpha_bf = sb("alpha_bf", [P, CG, 4], BF16)
+        weight_bf = sb("weight_bf", [P, CG, 4], BF16)
+        weight_col = sb("weight_col", [P, CG, 4], F32)
+        offset_col = sb("offset_col", [P, CG, 4], F32)
+
+        def p_scale(c, k):
+            return ps_first[:, k, c * G : (c + 1) * G] if c < 2 else ps_last[:, k, :]
+
+        def load_words(tile, src, lo, hi):
+            nc.sync.dma_start(
+                out=tile[:].bitcast(I32), in_=src.rearrange("k p n -> p k n")[:, :, 2 * lo : 2 * hi].bitcast(I32)
+            )
+
+        def load_scales(tile, src, lo, hi):
+            for q in range(4):
+                nc.sync.dma_start(
+                    out=tile[32 * q : 32 * q + 4, :, :].bitcast(I32),
+                    in_=src.rearrange("k r n -> r k n")[4 * q : 4 * q + 4, :, lo:hi].bitcast(I32),
+                )
+
+        def load_shifts(g):
+            rows = shifts[g * G : (g + 1) * G, :].rearrange("(u t e) m -> e u t m", t=4, e=4)
+            for e in range(4):
+                nc.sync.dma_start(out=s_raw[g][e:P:4, :, :], in_=rows[e])
+
+        def clear(eng, tile):
+            eng.memset(tile[:].rearrange("p k n -> p (k n)").bitcast(I32), 0)
+
+        def sort_tech(g):
+            raw_w, raw_s, lo = (t_raw_first, ts_raw_first, 0) if g == 0 else (t_raw_rest, ts_raw_rest, (g - 1) * G)
+            nc.vector.tensor_copy(
+                out=t_scales[g][:].bitcast(I32).rearrange("p k (t u) -> p k t u", t=4),
+                in_=raw_s[:, :, lo : lo + G].bitcast(I32).rearrange("p k (u t) -> p k t u", t=4),
+            )
+            for k in range(KP):
+                nc.vector.tensor_copy(
+                    out=t_words[g][:, k, :].bitcast(I32).rearrange("p (t u w) -> p t u w", t=4, w=2),
+                    in_=raw_w[:, k, 2 * lo : 2 * (lo + G)].bitcast(I32).rearrange("p (u t w) -> p t u w", t=4, w=2),
+                )
+
+        grouped = {}
+
+        def interleave(key, rows, width):
+            tile = stage.tile([P, width, 4], BF16, name="grouped", align_bytes=256)
+            grouped[key] = tile
+            nc.vector.tensor_copy(
+                out=tile[:].rearrange("p (c i) t -> p c t i", i=4),
+                in_=rows.rearrange("p t (c i) -> p c t i", i=4),
+            )
+
+        def quantise(key, codes, scales):
+            nc.vector.quantize_mx(
+                out=codes.bitcast(FP8X4), scales=scales, in_=grouped[key][:].rearrange("p c t -> p (c t)")
+            )
+
+        def s_i(g):
+            interleave(("s", g), s_raw[g][:], M)
+
+        def s_q(g):
+            quantise(("s", g), s_codes[g][:], s_scales[g][:])
+
+        def d_i(c, g):
+            interleave(("d", c, g), d_rows[c, g][:], G)
+
+        def d_q(c, g):
+            quantise(("d", c, g), d_codes[c, g][:], d_scales[c, g][:])
+
+        def slopes(c, g):
+            for t in range(4):
+                bank = psum.tile([P, G], F32, name="bank")
+                for k in range(KP):
+                    nc.tensor.matmul_mx(
+                        out=bank[:],
+                        lhsT=t_words[g][:, k, 2 * P * t : 2 * P * (t + 1)].bitcast(FP4X4),
+                        lhsT_scale=t_scales[g][:, k, P * t : P * (t + 1)],
+                        rhs=p_words[c][:, k, :].bitcast(FP4X4),
+                        rhs_scale=p_scale(c, k),
+                        start=(k == 0),
+                        stop=(k == KP - 1),
+                    )
+                nc.scalar.activation(
+                    out=d_rows[c, g][:, t, :].rearrange("p (j m) -> p j m", j=4),
+                    in_=bank[:].rearrange("p (m j) -> p j m", j=4),
+                    func=IDENT,
+                    bias=cost_col[:, t, g : g + 1],
+                    scale=-1.0,
+                )
+
+        pieces = [(0, 0, M), (1, 0, M), (2, 0, 256), (2, 256, 128), (2, 384, 128)]
+        y = [sb("y%d" % n, [P, 4, w], F32) for n, (c, lo, w) in enumerate(pieces)]
+        y_codes = sb("y_codes", [P, CG, M], U32)
+        y_scales = sb("y_scales", [P, CG, M], U8)
+
+        def values(n, j, on_vector=False):
+            c, lo, w = pieces[n]
+            bank = psum.tile([P, w], F32, name="bank")
+            for g in range(FG):
+                nc.tensor.matmul_mx(
+                    out=bank[:],
+                    lhsT=d_codes[c, g][:, P * j : P * (j + 1)].bitcast(FP8X4),
+                    lhsT_scale=d_scales[c, g][:, P * j : P * (j + 1)],
+                    rhs=s_codes[g][:, lo : lo + w].bitcast(FP8X4),
+                    rhs_scale=s_scales[g][:, lo : lo + w],
+                    start=(g == 0),
+                    stop=(g == FG - 1),
+                )
+            if on_vector:
+                nc.vector.tensor_scalar(
+                    out=y[n][:, j, :],
+                    in0=bank[:],
+                    scalar1=weight_col[:, c, j : j + 1],
+                    scalar2=offset_col[:, c, j : j + 1],
+                    op0=MULT,
+                    op1=ADD,
+                )
+            else:
+                nc.scalar.activation(
+                    out=y[n][:, j, :],
+                    in_=bank[:],
+                    func=IDENT,
+                    bias=offset_col[:, c, j : j + 1],
+                    scale=weight_col[:, c, j : j + 1],
+                )
+
+        def store_y(n):
+            c, lo, w = pieces[n]
+            nc.sync.dma_start(
+                out=out_0[c * G : (c + 1) * G, lo : lo + w].rearrange("(p j) m -> p j m", j=4), in_=y[n][:]
+            )
+
+        def y_i(n):
+            interleave(("y", n), y[n][:], pieces[n][2])
+
+        def y_q(n):
+            c, lo, w = pieces[n]
+            quantise(("y", n), y_codes[:, c, lo : lo + w], y_scales[:, c, lo : lo + w])
+
+        def store_codes(c, lo, hi):
+            nc.sync.dma_start(
+                out=out_1[c].rearrange("p m t -> p (m t)")[:, 4 * lo : 4 * hi].bitcast(I32),
+                in_=y_codes[:, c, lo:hi].bitcast(I32),
+            )
+
+        def store_scales(c0, c1, queues):
+            for q in range(4):
+                queues[q].dma_start(
+                    out=out_2.rearrange("c r m -> r c m")[4 * q : 4 * q + 4, c0:c1, :].bitcast(I32),
+                    in_=y_scales[32 * q : 32 * q + 4, c0:c1, :].bitcast(I32),
+                )
+
+        clear(nc.vector, ts_raw_first)
+        clear(nc.vector, ps_first)
+        nc.vector.memset(cost_sorted[:], 0.0)
+        clear(nc.vector, ts_raw_rest)
+        clear(nc.vector, ps_last)
+        make_identity(nc, ident[:])
+
+        nc.sync.dma_start(out=cost_row[:], in_=cost.rearrange("(g n) -> g n", n=G))
+        load_words(t_raw_first, tech_words, 0, G)
+        load_scales(ts_raw_first, tech_scales, 0, G)
+        load_words(p_words[0], duals_words, 0, G)
+        load_scales(ps_first, duals_scales, 0, 2 * G)
+        load_shifts(0)
+        load_words(p_words[1], duals_words, G, 2 * G)
+        load_words(t_raw_rest, tech_words, G, F)
+        load_scales(ts_raw_rest, tech_scales, G, F)
+        load_shifts(1)
+        load_shifts(2)
+        load_shifts(3)
+        load_words(p_words[2], duals_words, 2 * G, C)
+        load_scales(ps_last, duals_scales, 2 * G, C)
+        nc.sync.dma_start(out=weight_bf[:], in_=weight.rearrange("(c p j) -> p c j", p=P, j=4))
+        nc.sync.dma_start(out=alpha_bf[:], in_=alpha.rearrange("(c p j) -> p c j", p=P, j=4))
+
+        nc.vector.tensor_copy(
+            out=cost_sorted[0:FG, :, :].rearrange("g t (u e) -> g t u e", e=4),
+            in_=cost_row[:].rearrange("g (u t e) -> g t u e", t=4, e=4),
+        )
+        cost_bank = psum.tile([P, 4, P], BF16, name="bank")
+        for t in range(4):
+            nc.tensor.transpose(cost_bank[:, t, :], cost_sorted[:, t, :], ident[:])
+        nc.scalar.activation(out=cost_col[:], in_=cost_bank[:, :, 0:FG], func=IDENT)
+        nc.gpsimd.tensor_copy(out=weight_col[:], in_=weight_bf[:])
+        nc.gpsimd.tensor_tensor(out=offset_col[:], in0=weight_bf[:], in1=alpha_bf[:], op=MULT)
+
+        sort_tech(0)
+        slopes(0, 0)
+        s_i(0)
+        slopes(1, 0)
+        sort_tech(1)
+        s_q(0)
+        d_i(0, 0)
+        sort_tech(2)
+        d_q(0, 0)
+        slopes(0, 1)
+        s_i(1)
+        sort_tech(3)
+        s_q(1)
+        slopes(0, 2)
+        s_i(2)
+        d_i(0, 1)
+        s_q(2)
+        s_i(3)
+        d_q(0, 1)
+        slopes(0, 3)
+        d_i(0, 2)
+        s_q(3)
+        d_i(1, 0)
+        d_q(0, 2)
+        slopes(1, 1)
+        d_i(0, 3)
+        d_q(1, 0)
+        slopes(1, 2)
+        d_i(1, 1)
+        d_q(0, 3)
+        slopes(1, 3)
+        d_i(1, 2)
+        d_q(1, 1)
+        slopes(2, 0)
+        d_i(1, 3)
+        d_q(1, 2)
+        values(0, 0)
+        values(0, 1)
+        slopes(2, 1)
+        d_i(2, 0)
+        d_q(1, 3)
+        values(0, 2)
+        values(0, 3)
+        store_y(0)
+        d_i(2, 1)
+        d_q(2, 0)
+        slopes(2, 2)
+        y_i(0)
+        d_q(2, 1)
+        slopes(2, 3)
+        d_i(2, 2)
+        y_q(0)
+        store_codes(0, 0, M)
+        for j in range(4):
+            values(1, j)
+        store_y(1)
+        d_i(2, 3)
+        d_q(2, 2)
+        d_q(2, 3)
+        y_i(1)
+        y_q(1)
+        store_codes(1, 0, M)
+        store_scales(0, 2, [nc.sync] * 4)
+        for j in range(4):
+            values(2, j)
+        store_y(2)
+        y_i(2)
+        y_q(2)
+        store_codes(2, 0, 256)
+        for j in range(4):
+            values(3, j)
+        store_y(3)
+        y_i(3)
+        y_q(3)
+        for j in range(4):
+            values(4, j)
+        store_y(4)
+        y_i(4)
+        y_q(4)
+        store_codes(2, 256, M)
+        store_scales(2, 3, [nc.scalar, nc.sync, nc.scalar, nc.sync])

@@ -30,7 +30,7 @@ def tile_benders_cut_values_k5_kernel(
     nc = tc.nc
     with ExitStack() as ctx:
         keep = ctx.enter_context(tc.tile_pool(name="keep", bufs=1))
-        stage = ctx.enter_context(tc.tile_pool(name="stage", bufs=3))
+        stage = ctx.enter_context(tc.tile_pool(name="stage", bufs=4))
         psum = ctx.enter_context(tc.psum_pool(name="psum", bufs=8))
         ctx.enter_context(tc.manual_schedule())
 
@@ -38,7 +38,8 @@ def tile_benders_cut_values_k5_kernel(
             return keep.tile(shape, dtype, name=name, align_bytes=256)
 
         t_raw_first = sb("t_raw_first", [P, KP, 2 * G], U8)
-        t_raw_rest = sb("t_raw_rest", [P, KP, 2 * (F - G)], U8)
+        t_raw_second = sb("t_raw_second", [P, KP, 2 * G], U8)
+        t_raw_rest = sb("t_raw_rest", [P, KP, 2 * (F - 2 * G)], U8)
         ts_raw_first = sb("ts_raw_first", [P, KP, G], U8)
         ts_raw_rest = sb("ts_raw_rest", [P, KP, F - G], U8)
         t_words = [sb("t_words%d" % g, [P, KP, 2 * G], U8) for g in range(FG)]
@@ -69,11 +70,11 @@ def tile_benders_cut_values_k5_kernel(
                 out=tile[:].bitcast(I32), in_=src.rearrange("k p n -> p k n")[:, :, 2 * lo : 2 * hi].bitcast(I32)
             )
 
-        def load_scales(tile, src, lo, hi):
-            for q in range(4):
-                nc.sync.dma_start(
-                    out=tile[32 * q : 32 * q + 4, :, :].bitcast(I32),
-                    in_=src.rearrange("k r n -> r k n")[4 * q : 4 * q + 4, :, lo:hi].bitcast(I32),
+        def load_scales(tile, src, lo, hi, queue=nc.sync):
+            for r in range(4):
+                queue.dma_start(
+                    out=tile[r:P:32, :, :].bitcast(I32),
+                    in_=src.rearrange("k (q r) n -> r q k n", r=4)[r, :, :, lo:hi].bitcast(I32),
                 )
 
         def load_shifts(g):
@@ -85,7 +86,8 @@ def tile_benders_cut_values_k5_kernel(
             eng.memset(tile[:].rearrange("p k n -> p (k n)").bitcast(I32), 0)
 
         def sort_tech(g):
-            raw_w, raw_s, lo = (t_raw_first, ts_raw_first, 0) if g == 0 else (t_raw_rest, ts_raw_rest, (g - 1) * G)
+            raw_s, lo = (ts_raw_first, 0) if g == 0 else (ts_raw_rest, (g - 1) * G)
+            raw_w, wo = [(t_raw_first, 0), (t_raw_second, 0), (t_raw_rest, 0), (t_raw_rest, G)][g]
             nc.vector.tensor_copy(
                 out=t_scales[g][:].bitcast(I32).rearrange("p k (t u) -> p k t u", t=4),
                 in_=raw_s[:, :, lo : lo + G].bitcast(I32).rearrange("p k (u t) -> p k t u", t=4),
@@ -93,7 +95,7 @@ def tile_benders_cut_values_k5_kernel(
             for k in range(KP):
                 nc.vector.tensor_copy(
                     out=t_words[g][:, k, :].bitcast(I32).rearrange("p (t u w) -> p t u w", t=4, w=2),
-                    in_=raw_w[:, k, 2 * lo : 2 * (lo + G)].bitcast(I32).rearrange("p (u t w) -> p t u w", t=4, w=2),
+                    in_=raw_w[:, k, 2 * wo : 2 * (wo + G)].bitcast(I32).rearrange("p (u t w) -> p t u w", t=4, w=2),
                 )
 
         grouped = {}
@@ -118,7 +120,12 @@ def tile_benders_cut_values_k5_kernel(
             quantise(("s", g), s_codes[g][:], s_scales[g][:])
 
         def d_i(c, g):
-            interleave(("d", c, g), d_rows[c, g][:], G)
+            tile = stage.tile([P, G, 4], BF16, name="grouped", align_bytes=256)
+            grouped["d", c, g] = tile
+            nc.vector.tensor_copy(
+                out=tile[:].rearrange("p (e x i) t -> p x e t i", e=2, i=4),
+                in_=d_rows[c, g][:].rearrange("p t (x i e) -> p x e t i", e=2, i=4),
+            )
 
         def d_q(c, g):
             quantise(("d", c, g), d_codes[c, g][:], d_scales[c, g][:])
@@ -137,14 +144,14 @@ def tile_benders_cut_values_k5_kernel(
                         stop=(k == KP - 1),
                     )
                 nc.scalar.activation(
-                    out=d_rows[c, g][:, t, :].rearrange("p (j m) -> p j m", j=4),
-                    in_=bank[:].rearrange("p (m j) -> p j m", j=4),
+                    out=d_rows[c, g][:, t, :].rearrange("p (h m e) -> p h m e", h=2, e=2),
+                    in_=bank[:].rearrange("p (m h e) -> p h m e", h=2, e=2),
                     func=IDENT,
                     bias=cost_col[:, t, g : g + 1],
                     scale=-1.0,
                 )
 
-        pieces = [(0, 0, M), (1, 0, M), (2, 0, 256), (2, 256, 128), (2, 384, 128)]
+        pieces = [(0, 0, M), (1, 0, 256), (1, 256, 256), (2, 0, 256), (2, 256, 128), (2, 384, 128)]
         y = [sb("y%d" % n, [P, 4, w], F32) for n, (c, lo, w) in enumerate(pieces)]
         y_codes = sb("y_codes", [P, CG, M], U32)
         y_scales = sb("y_scales", [P, CG, M], U8)
@@ -152,11 +159,12 @@ def tile_benders_cut_values_k5_kernel(
         def values(n, j, on_vector=False):
             c, lo, w = pieces[n]
             bank = psum.tile([P, w], F32, name="bank")
+            col = P * (2 * (j % 2) + j // 2)
             for g in range(FG):
                 nc.tensor.matmul_mx(
                     out=bank[:],
-                    lhsT=d_codes[c, g][:, P * j : P * (j + 1)].bitcast(FP8X4),
-                    lhsT_scale=d_scales[c, g][:, P * j : P * (j + 1)],
+                    lhsT=d_codes[c, g][:, col : col + P].bitcast(FP8X4),
+                    lhsT_scale=d_scales[c, g][:, col : col + P],
                     rhs=s_codes[g][:, lo : lo + w].bitcast(FP8X4),
                     rhs_scale=s_scales[g][:, lo : lo + w],
                     start=(g == 0),
@@ -200,10 +208,10 @@ def tile_benders_cut_values_k5_kernel(
             )
 
         def store_scales(c0, c1, queues):
-            for q in range(4):
-                queues[q].dma_start(
-                    out=out_2.rearrange("c r m -> r c m")[4 * q : 4 * q + 4, c0:c1, :].bitcast(I32),
-                    in_=y_scales[32 * q : 32 * q + 4, c0:c1, :].bitcast(I32),
+            for r in range(4):
+                queues[r].dma_start(
+                    out=out_2.rearrange("c (q r) m -> r q c m", r=4)[r, :, c0:c1, :].bitcast(I32),
+                    in_=y_scales[r:P:32, c0:c1, :].bitcast(I32),
                 )
 
         clear(nc.vector, ts_raw_first)
@@ -215,18 +223,19 @@ def tile_benders_cut_values_k5_kernel(
 
         nc.sync.dma_start(out=cost_row[:], in_=cost.rearrange("(g n) -> g n", n=G))
         load_words(t_raw_first, tech_words, 0, G)
-        load_scales(ts_raw_first, tech_scales, 0, G)
+        load_scales(ts_raw_first, tech_scales, 0, G, nc.scalar)
         load_words(p_words[0], duals_words, 0, G)
         load_scales(ps_first, duals_scales, 0, 2 * G)
         load_shifts(0)
         load_words(p_words[1], duals_words, G, 2 * G)
-        load_words(t_raw_rest, tech_words, G, F)
         load_scales(ts_raw_rest, tech_scales, G, F)
+        load_words(t_raw_second, tech_words, G, 2 * G)
+        load_words(t_raw_rest, tech_words, 2 * G, F)
         load_shifts(1)
         load_shifts(2)
         load_shifts(3)
-        load_words(p_words[2], duals_words, 2 * G, C)
         load_scales(ps_last, duals_scales, 2 * G, C)
+        load_words(p_words[2], duals_words, 2 * G, C)
         nc.sync.dma_start(out=weight_bf[:], in_=weight.rearrange("(c p j) -> p c j", p=P, j=4))
         nc.sync.dma_start(out=alpha_bf[:], in_=alpha.rearrange("(c p j) -> p c j", p=P, j=4))
 
@@ -242,83 +251,86 @@ def tile_benders_cut_values_k5_kernel(
         nc.gpsimd.tensor_tensor(out=offset_col[:], in0=weight_bf[:], in1=alpha_bf[:], op=MULT)
 
         sort_tech(0)
-        slopes(0, 0)
         s_i(0)
-        slopes(1, 0)
-        sort_tech(1)
         s_q(0)
+        sort_tech(1)
+        slopes(0, 0)
         d_i(0, 0)
         sort_tech(2)
         d_q(0, 0)
-        slopes(0, 1)
-        s_i(1)
         sort_tech(3)
+        s_i(1)
+        slopes(1, 0)
+        d_i(1, 0)
         s_q(1)
-        slopes(0, 2)
         s_i(2)
+        d_q(1, 0)
+        slopes(0, 1)
         d_i(0, 1)
         s_q(2)
         s_i(3)
         d_q(0, 1)
-        slopes(0, 3)
-        d_i(0, 2)
-        s_q(3)
-        d_i(1, 0)
-        d_q(0, 2)
         slopes(1, 1)
-        d_i(0, 3)
-        d_q(1, 0)
-        slopes(1, 2)
         d_i(1, 1)
+        s_q(3)
+        slopes(0, 2)
+        d_i(0, 2)
+        d_q(1, 1)
+        slopes(0, 3)
+        d_i(0, 3)
+        d_q(0, 2)
+        slopes(1, 2)
+        d_i(1, 2)
         d_q(0, 3)
         slopes(1, 3)
-        d_i(1, 2)
-        d_q(1, 1)
-        slopes(2, 0)
         d_i(1, 3)
         d_q(1, 2)
-        values(0, 0)
-        values(0, 1)
-        slopes(2, 1)
+        slopes(2, 0)
         d_i(2, 0)
         d_q(1, 3)
-        values(0, 2)
-        values(0, 3)
-        store_y(0)
+        slopes(2, 1)
         d_i(2, 1)
         d_q(2, 0)
-        slopes(2, 2)
+        for j in range(4):
+            values(0, j)
+        store_y(0)
         y_i(0)
         d_q(2, 1)
-        slopes(2, 3)
+        slopes(2, 2)
         d_i(2, 2)
         y_q(0)
-        store_codes(0, 0, M)
+        store_codes(0, 0, 512)
+        slopes(2, 3)
+        d_i(2, 3)
+        d_q(2, 2)
         for j in range(4):
             values(1, j)
         store_y(1)
-        d_i(2, 3)
-        d_q(2, 2)
-        d_q(2, 3)
         y_i(1)
+        d_q(2, 3)
         y_q(1)
-        store_codes(1, 0, M)
-        store_scales(0, 2, [nc.sync] * 4)
         for j in range(4):
             values(2, j)
         store_y(2)
         y_i(2)
         y_q(2)
-        store_codes(2, 0, 256)
+        store_codes(1, 0, 512)
+        store_scales(0, 2, [nc.sync] * 4)
         for j in range(4):
             values(3, j)
         store_y(3)
         y_i(3)
         y_q(3)
+        store_codes(2, 0, 256)
         for j in range(4):
             values(4, j)
         store_y(4)
         y_i(4)
         y_q(4)
-        store_codes(2, 256, M)
+        for j in range(4):
+            values(5, j)
+        store_y(5)
+        y_i(5)
+        y_q(5)
+        store_codes(2, 256, 512)
         store_scales(2, 3, [nc.scalar, nc.sync, nc.scalar, nc.sync])

@@ -92,11 +92,10 @@ def tile_benders_cut_values_k5_kernel(
                 out=t_scales[g][:].bitcast(I32).rearrange("p k (t u) -> p k t u", t=4),
                 in_=raw_s[:, :, lo : lo + G].bitcast(I32).rearrange("p k (u t) -> p k t u", t=4),
             )
-            for k in range(KP):
-                nc.vector.tensor_copy(
-                    out=t_words[g][:, k, :].bitcast(I32).rearrange("p (t u w) -> p t u w", t=4, w=2),
-                    in_=raw_w[:, k, 2 * wo : 2 * (wo + G)].bitcast(I32).rearrange("p (u t w) -> p t u w", t=4, w=2),
-                )
+            nc.vector.tensor_copy(
+                out=t_words[g][:].bitcast(I32).rearrange("p k (t u w) -> p k t u w", t=4, w=2),
+                in_=raw_w[:, :, 2 * wo : 2 * (wo + G)].bitcast(I32).rearrange("p k (u t w) -> p k t u w", t=4, w=2),
+            )
 
         grouped = {}
 
@@ -222,8 +221,8 @@ def tile_benders_cut_values_k5_kernel(
         make_identity(nc, ident[:])
 
         nc.sync.dma_start(out=cost_row[:], in_=cost.rearrange("(g n) -> g n", n=G))
-        load_words(t_raw_first, tech_words, 0, G)
         load_scales(ts_raw_first, tech_scales, 0, G, nc.scalar)
+        load_words(t_raw_first, tech_words, 0, G)
         load_words(p_words[0], duals_words, 0, G)
         load_scales(ps_first, duals_scales, 0, 2 * G)
         load_shifts(0)
@@ -251,37 +250,37 @@ def tile_benders_cut_values_k5_kernel(
         nc.gpsimd.tensor_tensor(out=offset_col[:], in0=weight_bf[:], in1=alpha_bf[:], op=MULT)
 
         sort_tech(0)
+        slopes(0, 0)
         s_i(0)
         s_q(0)
         sort_tech(1)
-        slopes(0, 0)
+        slopes(1, 0)
         d_i(0, 0)
         sort_tech(2)
         d_q(0, 0)
         sort_tech(3)
-        s_i(1)
-        slopes(1, 0)
-        d_i(1, 0)
-        s_q(1)
-        s_i(2)
-        d_q(1, 0)
         slopes(0, 1)
+        s_i(1)
         d_i(0, 1)
-        s_q(2)
-        s_i(3)
-        d_q(0, 1)
+        s_q(1)
         slopes(1, 1)
-        d_i(1, 1)
-        s_q(3)
+        s_i(2)
+        d_q(0, 1)
+        s_i(3)
+        s_q(2)
         slopes(0, 2)
         d_i(0, 2)
-        d_q(1, 1)
+        s_q(3)
         slopes(0, 3)
         d_i(0, 3)
         d_q(0, 2)
-        slopes(1, 2)
-        d_i(1, 2)
+        d_i(1, 0)
         d_q(0, 3)
+        slopes(1, 2)
+        d_i(1, 1)
+        d_q(1, 0)
+        d_i(1, 2)
+        d_q(1, 1)
         slopes(1, 3)
         d_i(1, 3)
         d_q(1, 2)
@@ -303,16 +302,16 @@ def tile_benders_cut_values_k5_kernel(
         slopes(2, 3)
         d_i(2, 3)
         d_q(2, 2)
+        d_q(2, 3)
         for j in range(4):
             values(1, j)
         store_y(1)
         y_i(1)
-        d_q(2, 3)
-        y_q(1)
         for j in range(4):
             values(2, j)
         store_y(2)
         y_i(2)
+        y_q(1)
         y_q(2)
         store_codes(1, 0, 512)
         store_scales(0, 2, [nc.sync] * 4)
@@ -326,11 +325,11 @@ def tile_benders_cut_values_k5_kernel(
             values(4, j)
         store_y(4)
         y_i(4)
-        y_q(4)
         for j in range(4):
             values(5, j)
         store_y(5)
         y_i(5)
+        y_q(4)
         y_q(5)
         store_codes(2, 256, 512)
         store_scales(2, 3, [nc.scalar, nc.sync, nc.scalar, nc.sync])

@@ -3,8 +3,8 @@ from contextlib import ExitStack
 import concourse.mybir as mybir
 from concourse.masks import make_identity
 
-C, K, F, M = 1536, 1024, 2048, 512
-FLOPS = 2 * K * C * F + 2 * C * F * M
+CUTS, CONSTRAINTS, VARIABLES, PLANS = 1536, 1024, 2048, 512
+FLOPS = 2 * CONSTRAINTS * CUTS * VARIABLES + 2 * CUTS * VARIABLES * PLANS
 
 F32 = mybir.dt.float32
 BF16 = mybir.dt.bfloat16
@@ -13,15 +13,24 @@ U32 = mybir.dt.uint32
 U8 = mybir.dt.uint8
 FP8X4 = mybir.dt.float8_e4m3fn_x4
 FP4X4 = mybir.dt.float4_e2m1fn_x4
-IDENT = mybir.ActivationFunctionType.Identity
-MULT = mybir.AluOpType.mult
-ADD = mybir.AluOpType.add
+IDENTITY = mybir.ActivationFunctionType.Identity
 
 P = 128
-G = 512
-KP = K // G
-FG = F // G
-CG = C // G
+PACK = 4
+GROUP = P * PACK
+K_GROUPS = CONSTRAINTS // GROUP
+VAR_GROUPS = VARIABLES // GROUP
+CUT_GROUPS = CUTS // GROUP
+FP4_BYTES = 2
+QUADRANT = 32
+RUN = 4
+
+SHIFT_SETS = [(0,), (1,), (2, 3)]
+SLOPE_SETS = [(c, gs) for c in (0, 1) for gs in ((0, 1), (2, 3))] + [(2, (g,)) for g in range(VAR_GROUPS)]
+
+PIECES = [(0, 0, 512), (1, 0, 256), (1, 256, 256), (2, 0, 256), (2, 256, 128), (2, 384, 128)]
+
+SINGLE_BUFS, PAIR_BUFS = 4, 3
 
 
 def tile_benders_cut_values_k5_kernel(
@@ -30,306 +39,312 @@ def tile_benders_cut_values_k5_kernel(
     nc = tc.nc
     with ExitStack() as ctx:
         keep = ctx.enter_context(tc.tile_pool(name="keep", bufs=1))
-        stage = ctx.enter_context(tc.tile_pool(name="stage", bufs=4))
+        stage = ctx.enter_context(tc.tile_pool(name="stage", bufs=SINGLE_BUFS))
         psum = ctx.enter_context(tc.psum_pool(name="psum", bufs=8))
         ctx.enter_context(tc.manual_schedule())
 
-        def sb(name, shape, dtype):
+        def kept(name, shape, dtype):
             return keep.tile(shape, dtype, name=name, align_bytes=256)
 
-        t_raw_first = sb("t_raw_first", [P, KP, 2 * G], U8)
-        t_raw_second = sb("t_raw_second", [P, KP, 2 * G], U8)
-        t_raw_rest = sb("t_raw_rest", [P, KP, 2 * (F - 2 * G)], U8)
-        ts_raw_first = sb("ts_raw_first", [P, KP, G], U8)
-        ts_raw_rest = sb("ts_raw_rest", [P, KP, F - G], U8)
-        t_words = [sb("t_words%d" % g, [P, KP, 2 * G], U8) for g in range(FG)]
-        t_scales = [sb("t_scales%d" % g, [P, KP, G], U8) for g in range(FG)]
-        p_words = [sb("p_words%d" % c, [P, KP, 2 * G], U8) for c in range(CG)]
-        ps_first = sb("ps_first", [P, KP, 2 * G], U8)
-        ps_last = sb("ps_last", [P, KP, G], U8)
-        s_raw = [sb("s_raw%d" % g, [P, 4, M], BF16) for g in range(FG)]
-        s_codes = [sb("s_codes%d" % g, [P, M], U32) for g in range(FG)]
-        s_scales = [sb("s_scales%d" % g, [P, M], U8) for g in range(FG)]
-        d_rows = {(c, g): sb("d_rows%d_%d" % (c, g), [P, 4, G], BF16) for c in range(CG) for g in range(FG)}
-        d_codes = {(c, g): sb("d_codes%d_%d" % (c, g), [P, G], U32) for c in range(CG) for g in range(FG)}
-        d_scales = {(c, g): sb("d_scales%d_%d" % (c, g), [P, G], U8) for c in range(CG) for g in range(FG)}
-        cost_row = sb("cost_row", [FG, G], BF16)
-        cost_sorted = sb("cost_sorted", [P, 4, P], BF16)
-        cost_col = sb("cost_col", [P, 4, FG], F32)
-        ident = sb("ident", [P, P], BF16)
-        alpha_bf = sb("alpha_bf", [P, CG, 4], BF16)
-        weight_bf = sb("weight_bf", [P, CG, 4], BF16)
-        weight_col = sb("weight_col", [P, CG, 4], F32)
-        offset_col = sb("offset_col", [P, CG, 4], F32)
+        tech_raw = [kept("tech_raw%d" % n, [P, K_GROUPS, w * FP4_BYTES * GROUP], U8) for n, w in enumerate((1, 1, 2))]
+        tech_scale_raw = [kept("tech_scale_raw%d" % n, [P, K_GROUPS, w * GROUP], U8) for n, w in enumerate((1, 3))]
+        tech_sorted = [
+            kept("tech_sorted%d" % n, [P, K_GROUPS, w * FP4_BYTES * GROUP], U8) for n, w in enumerate((1, 1, 2))
+        ]
+        tech_scale_sorted = [
+            kept("tech_scale_sorted%d" % n, [P, K_GROUPS, w * GROUP], U8) for n, w in enumerate((1, 3))
+        ]
+        tech_of_group = tech_sorted[:2] + [
+            tech_sorted[2][:, :, h * FP4_BYTES * GROUP : (h + 1) * FP4_BYTES * GROUP] for h in range(2)
+        ]
+        tech_scale_of_group = tech_scale_sorted[:1] + [
+            tech_scale_sorted[1][:, :, h * GROUP : (h + 1) * GROUP] for h in range(3)
+        ]
+        duals = [kept("duals%d" % c, [P, K_GROUPS, FP4_BYTES * GROUP], U8) for c in range(CUT_GROUPS)]
+        duals_scale = [kept("duals_scale%d" % n, [P, K_GROUPS, w * GROUP], U8) for n, w in enumerate((2, 1))]
+        duals_scale_of_group = [duals_scale[0][:, :, h * GROUP : (h + 1) * GROUP] for h in range(2)] + duals_scale[1:]
 
-        def p_scale(c, k):
-            return ps_first[:, k, c * G : (c + 1) * G] if c < 2 else ps_last[:, k, :]
+        shift_rows, shift_codes, shift_scales = {}, {}, {}
+        for gs in SHIFT_SETS:
+            shift_rows[gs] = kept("shift_rows%d" % gs[0], [P, PACK, len(gs), PLANS], BF16)
+            shift_codes[gs] = kept("shift_codes%d" % gs[0], [P, len(gs) * PLANS], U32)
+            shift_scales[gs] = kept("shift_scales%d" % gs[0], [P, len(gs) * PLANS], U8)
+        slope_rows, slope_codes, slope_scales = {}, {}, {}
+        for c, gs in SLOPE_SETS:
+            slope_rows[c, gs] = kept("slope_rows%d_%d" % (c, gs[0]), [P, PACK, len(gs), GROUP], BF16)
+            slope_codes[c, gs] = kept("slope_codes%d_%d" % (c, gs[0]), [P, len(gs) * GROUP], U32)
+            slope_scales[c, gs] = kept("slope_scales%d_%d" % (c, gs[0]), [P, len(gs) * GROUP], U8)
+        shift_set_of = {g: gs for gs in SHIFT_SETS for g in gs}
+        slope_set_of = {(c, g): gs for c, gs in SLOPE_SETS for g in gs}
 
-        def load_words(tile, src, lo, hi):
-            nc.sync.dma_start(
-                out=tile[:].bitcast(I32), in_=src.rearrange("k p n -> p k n")[:, :, 2 * lo : 2 * hi].bitcast(I32)
-            )
+        cost_rows = kept("cost_rows", [VAR_GROUPS, GROUP], BF16)
+        cost_sorted = kept("cost_sorted", [P, PACK, P], BF16)
+        cost_col = kept("cost_col", [P, PACK, VAR_GROUPS], F32)
+        identity = kept("identity", [P, P], BF16)
+        alpha_bf = kept("alpha_bf", [P, CUT_GROUPS, PACK], BF16)
+        weight_bf = kept("weight_bf", [P, CUT_GROUPS, PACK], BF16)
+        weight_col = kept("weight_col", [P, CUT_GROUPS, PACK], F32)
+        offset_col = kept("offset_col", [P, CUT_GROUPS, PACK], F32)
+        y = [kept("y%d" % n, [P, PACK, width], F32) for n, (c, first, width) in enumerate(PIECES)]
+        y_codes = kept("y_codes", [P, CUT_GROUPS, PLANS], U32)
+        y_scales = kept("y_scales", [P, CUT_GROUPS, PLANS], U8)
 
-        def load_scales(tile, src, lo, hi, queue=nc.sync):
+        def flat_words(tile):
+            return tile[:].rearrange("p k n -> p (k n)").bitcast(I32)
+
+
+        def load_words(tile, src, first_group, groups):
+            cols = slice(FP4_BYTES * GROUP * first_group, FP4_BYTES * GROUP * (first_group + groups))
+            nc.sync.dma_start(out=tile[:].bitcast(I32), in_=src.rearrange("k p n -> p k n")[:, :, cols].bitcast(I32))
+
+        def load_scales(queue, tile, src, first_group, groups):
+            cols = slice(GROUP * first_group, GROUP * (first_group + groups))
             for r in range(4):
                 queue.dma_start(
-                    out=tile[r:P:32, :, :].bitcast(I32),
-                    in_=src.rearrange("k (q r) n -> r q k n", r=4)[r, :, :, lo:hi].bitcast(I32),
+                    out=tile[r:P:QUADRANT, :, :].bitcast(I32),
+                    in_=src.rearrange("k (q r) n -> r q k n", r=4)[r, :, :, cols].bitcast(I32),
                 )
 
         def load_shifts(g):
-            rows = shifts[g * G : (g + 1) * G, :].rearrange("(u t e) m -> e u t m", t=4, e=4)
+            gs = shift_set_of[g]
+            rows = shifts[g * GROUP : (g + 1) * GROUP, :].rearrange("(u t e) m -> e u t m", t=PACK, e=4)
             for e in range(4):
-                nc.sync.dma_start(out=s_raw[g][e:P:4, :, :], in_=rows[e])
+                nc.sync.dma_start(out=shift_rows[gs][e:P:4, :, gs.index(g), :], in_=rows[e])
 
-        def clear(eng, tile):
-            eng.memset(tile[:].rearrange("p k n -> p (k n)").bitcast(I32), 0)
 
-        def sort_tech(g):
-            raw_s, lo = (ts_raw_first, 0) if g == 0 else (ts_raw_rest, (g - 1) * G)
-            raw_w, wo = [(t_raw_first, 0), (t_raw_second, 0), (t_raw_rest, 0), (t_raw_rest, G)][g]
+        def sort_tech_scales(n):
             nc.vector.tensor_copy(
-                out=t_scales[g][:].bitcast(I32).rearrange("p k (t u) -> p k t u", t=4),
-                in_=raw_s[:, :, lo : lo + G].bitcast(I32).rearrange("p k (u t) -> p k t u", t=4),
-            )
-            nc.vector.tensor_copy(
-                out=t_words[g][:].bitcast(I32).rearrange("p k (t u w) -> p k t u w", t=4, w=2),
-                in_=raw_w[:, :, 2 * wo : 2 * (wo + G)].bitcast(I32).rearrange("p k (u t w) -> p k t u w", t=4, w=2),
+                out=flat_words(tech_scale_sorted[n]).rearrange("p (a t u) -> p a t u", t=PACK, u=32),
+                in_=flat_words(tech_scale_raw[n]).rearrange("p (a u t) -> p a t u", t=PACK, u=32),
             )
 
-        grouped = {}
+        def sort_tech_words(n):
+            nc.vector.tensor_copy(
+                out=flat_words(tech_sorted[n]).rearrange("p (a t u w) -> p a t u w", t=PACK, u=32, w=2),
+                in_=flat_words(tech_raw[n]).rearrange("p (a u t w) -> p a t u w", t=PACK, u=32, w=2),
+            )
+
+
+        interleaved = {}
+
+        def new_interleaved(key, shape, pair):
+            name, bufs = ("interleaved_pair", PAIR_BUFS) if pair else ("interleaved", SINGLE_BUFS)
+            interleaved[key] = stage.tile(shape, BF16, name=name, bufs=bufs, align_bytes=256)
 
         def interleave(key, rows, width):
-            tile = stage.tile([P, width, 4], BF16, name="grouped", align_bytes=256)
-            grouped[key] = tile
+            new_interleaved(key, [P, width, PACK], width > GROUP)
             nc.vector.tensor_copy(
-                out=tile[:].rearrange("p (c i) t -> p c t i", i=4),
-                in_=rows.rearrange("p t (c i) -> p c t i", i=4),
+                out=interleaved[key][:].rearrange("p (x i) t -> p x t i", i=RUN),
+                in_=rows.rearrange("p t (x i) -> p x t i", i=RUN),
             )
 
         def quantise(key, codes, scales):
             nc.vector.quantize_mx(
-                out=codes.bitcast(FP8X4), scales=scales, in_=grouped[key][:].rearrange("p c t -> p (c t)")
+                out=codes.bitcast(FP8X4), scales=scales, in_=interleaved[key][:].rearrange("p x t -> p (x t)")
             )
 
-        def s_i(g):
-            interleave(("s", g), s_raw[g][:], M)
+        def interleave_shifts(*gs):
+            interleave(("shifts", gs), shift_rows[gs][:].rearrange("p t g m -> p t (g m)"), len(gs) * PLANS)
 
-        def s_q(g):
-            quantise(("s", g), s_codes[g][:], s_scales[g][:])
+        def quantise_shifts(*gs):
+            quantise(("shifts", gs), shift_codes[gs][:], shift_scales[gs][:])
 
-        def d_i(c, g):
-            tile = stage.tile([P, G, 4], BF16, name="grouped", align_bytes=256)
-            grouped["d", c, g] = tile
-            nc.vector.tensor_copy(
-                out=tile[:].rearrange("p (e x i) t -> p x e t i", e=2, i=4),
-                in_=d_rows[c, g][:].rearrange("p t (x i e) -> p x e t i", e=2, i=4),
-            )
-
-        def d_q(c, g):
-            quantise(("d", c, g), d_codes[c, g][:], d_scales[c, g][:])
 
         def slopes(c, g):
-            for t in range(4):
-                bank = psum.tile([P, G], F32, name="bank")
-                for k in range(KP):
+            gs = slope_set_of[c, g]
+            for t in range(PACK):
+                bank = psum.tile([P, GROUP], F32, name="bank")
+                for k in range(K_GROUPS):
                     nc.tensor.matmul_mx(
                         out=bank[:],
-                        lhsT=t_words[g][:, k, 2 * P * t : 2 * P * (t + 1)].bitcast(FP4X4),
-                        lhsT_scale=t_scales[g][:, k, P * t : P * (t + 1)],
-                        rhs=p_words[c][:, k, :].bitcast(FP4X4),
-                        rhs_scale=p_scale(c, k),
+                        lhsT=tech_of_group[g][:, k, FP4_BYTES * P * t : FP4_BYTES * P * (t + 1)].bitcast(FP4X4),
+                        lhsT_scale=tech_scale_of_group[g][:, k, P * t : P * (t + 1)],
+                        rhs=duals[c][:, k, :].bitcast(FP4X4),
+                        rhs_scale=duals_scale_of_group[c][:, k, :],
                         start=(k == 0),
-                        stop=(k == KP - 1),
+                        stop=(k == K_GROUPS - 1),
                     )
                 nc.scalar.activation(
-                    out=d_rows[c, g][:, t, :].rearrange("p (h m e) -> p h m e", h=2, e=2),
-                    in_=bank[:].rearrange("p (m h e) -> p h m e", h=2, e=2),
-                    func=IDENT,
+                    out=slope_rows[c, gs][:, t, gs.index(g), :].rearrange("p (h m b) -> p h m b", h=2, b=2),
+                    in_=bank[:].rearrange("p (m h b) -> p h m b", h=2, b=2),
+                    func=IDENTITY,
                     bias=cost_col[:, t, g : g + 1],
                     scale=-1.0,
                 )
 
-        pieces = [(0, 0, M), (1, 0, 256), (1, 256, 256), (2, 0, 256), (2, 256, 128), (2, 384, 128)]
-        y = [sb("y%d" % n, [P, 4, w], F32) for n, (c, lo, w) in enumerate(pieces)]
-        y_codes = sb("y_codes", [P, CG, M], U32)
-        y_scales = sb("y_scales", [P, CG, M], U8)
+        def slope_views(c, part):
+            gs = slope_set_of[c, part[0]]
+            if ("slopes", c, gs) not in interleaved:
+                new_interleaved(("slopes", c, gs), [P, 2, len(gs), GROUP // 2, PACK], len(gs) > 1)
+            groups = slice(gs.index(part[0]), gs.index(part[0]) + len(part))
+            dst = interleaved["slopes", c, gs][:, :, groups, :, :].rearrange("p b g (x i) t -> p (g x) b t i", i=RUN)
+            src = slope_rows[c, gs][:, :, groups, :].rearrange("p t g (x i b) -> p (g x) b t i", b=2, i=RUN)
+            return dst, src
 
-        def values(n, j, on_vector=False):
-            c, lo, w = pieces[n]
-            bank = psum.tile([P, w], F32, name="bank")
-            col = P * (2 * (j % 2) + j // 2)
-            for g in range(FG):
-                nc.tensor.matmul_mx(
-                    out=bank[:],
-                    lhsT=d_codes[c, g][:, col : col + P].bitcast(FP8X4),
-                    lhsT_scale=d_scales[c, g][:, col : col + P],
-                    rhs=s_codes[g][:, lo : lo + w].bitcast(FP8X4),
-                    rhs_scale=s_scales[g][:, lo : lo + w],
-                    start=(g == 0),
-                    stop=(g == FG - 1),
-                )
-            if on_vector:
-                nc.vector.tensor_scalar(
-                    out=y[n][:, j, :],
-                    in0=bank[:],
-                    scalar1=weight_col[:, c, j : j + 1],
-                    scalar2=offset_col[:, c, j : j + 1],
-                    op0=MULT,
-                    op1=ADD,
-                )
-            else:
+        def interleave_slopes(c, *part):
+            dst, src = slope_views(c, part)
+            nc.vector.tensor_copy(out=dst, in_=src)
+
+        def interleave_slopes_shared(c, g):
+            dst, src = slope_views(c, (g,))
+            nc.scalar.activation(out=dst[:, :, 0, :, :], in_=src[:, :, 0, :, :], func=IDENTITY)
+            nc.vector.tensor_copy(out=dst[:, :, 1, :, :], in_=src[:, :, 1, :, :])
+
+        def quantise_slopes(c, *gs):
+            nc.vector.quantize_mx(
+                out=slope_codes[c, gs][:].bitcast(FP8X4),
+                scales=slope_scales[c, gs][:],
+                in_=interleaved["slopes", c, gs][:].rearrange("p b g n t -> p (b g n t)"),
+            )
+
+
+        def values(n):
+            c, first, width = PIECES[n]
+            for j in range(PACK):
+                bank = psum.tile([P, width], F32, name="bank")
+                for g in range(VAR_GROUPS):
+                    slope_set, shift_set = slope_set_of[c, g], shift_set_of[g]
+                    cut_col = P * (2 * len(slope_set) * (j % 2) + 2 * slope_set.index(g) + j // 2)
+                    plan_col = shift_set.index(g) * PLANS + first
+                    nc.tensor.matmul_mx(
+                        out=bank[:],
+                        lhsT=slope_codes[c, slope_set][:, cut_col : cut_col + P].bitcast(FP8X4),
+                        lhsT_scale=slope_scales[c, slope_set][:, cut_col : cut_col + P],
+                        rhs=shift_codes[shift_set][:, plan_col : plan_col + width].bitcast(FP8X4),
+                        rhs_scale=shift_scales[shift_set][:, plan_col : plan_col + width],
+                        start=(g == 0),
+                        stop=(g == VAR_GROUPS - 1),
+                    )
                 nc.scalar.activation(
                     out=y[n][:, j, :],
                     in_=bank[:],
-                    func=IDENT,
+                    func=IDENTITY,
                     bias=offset_col[:, c, j : j + 1],
                     scale=weight_col[:, c, j : j + 1],
                 )
-
-        def store_y(n):
-            c, lo, w = pieces[n]
             nc.sync.dma_start(
-                out=out_0[c * G : (c + 1) * G, lo : lo + w].rearrange("(p j) m -> p j m", j=4), in_=y[n][:]
+                out=out_0[c * GROUP : (c + 1) * GROUP, first : first + width].rearrange("(p j) m -> p j m", j=PACK),
+                in_=y[n][:],
             )
 
-        def y_i(n):
-            interleave(("y", n), y[n][:], pieces[n][2])
+        def interleave_y(n):
+            interleave(("y", n), y[n][:], PIECES[n][2])
 
-        def y_q(n):
-            c, lo, w = pieces[n]
-            quantise(("y", n), y_codes[:, c, lo : lo + w], y_scales[:, c, lo : lo + w])
+        def quantise_y(n):
+            c, first, width = PIECES[n]
+            quantise(("y", n), y_codes[:, c, first : first + width], y_scales[:, c, first : first + width])
 
-        def store_codes(c, lo, hi):
+        def store_codes(c, first, end):
             nc.sync.dma_start(
-                out=out_1[c].rearrange("p m t -> p (m t)")[:, 4 * lo : 4 * hi].bitcast(I32),
-                in_=y_codes[:, c, lo:hi].bitcast(I32),
+                out=out_1[c].rearrange("p m t -> p (m t)")[:, PACK * first : PACK * end].bitcast(I32),
+                in_=y_codes[:, c, first:end].bitcast(I32),
             )
 
-        def store_scales(c0, c1, queues):
+        def store_scales(first_group, end_group, queues):
             for r in range(4):
                 queues[r].dma_start(
-                    out=out_2.rearrange("c (q r) m -> r q c m", r=4)[r, :, c0:c1, :].bitcast(I32),
-                    in_=y_scales[r:P:32, c0:c1, :].bitcast(I32),
+                    out=out_2.rearrange("c (q r) m -> r q c m", r=4)[r, :, first_group:end_group, :].bitcast(I32),
+                    in_=y_scales[r:P:QUADRANT, first_group:end_group, :].bitcast(I32),
                 )
 
-        clear(nc.vector, ts_raw_first)
-        clear(nc.vector, ps_first)
+        nc.vector.memset(flat_words(tech_scale_raw[0]), 0)
+        nc.vector.memset(flat_words(duals_scale[0]), 0)
         nc.vector.memset(cost_sorted[:], 0.0)
-        clear(nc.vector, ts_raw_rest)
-        clear(nc.vector, ps_last)
-        make_identity(nc, ident[:])
+        nc.vector.memset(flat_words(tech_scale_raw[1]), 0)
+        nc.vector.memset(flat_words(duals_scale[1]), 0)
+        make_identity(nc, identity[:])
 
-        nc.sync.dma_start(out=cost_row[:], in_=cost.rearrange("(g n) -> g n", n=G))
-        load_scales(ts_raw_first, tech_scales, 0, G, nc.scalar)
-        load_words(t_raw_first, tech_words, 0, G)
-        load_words(p_words[0], duals_words, 0, G)
-        load_scales(ps_first, duals_scales, 0, 2 * G)
+        nc.sync.dma_start(out=cost_rows[:], in_=cost.rearrange("(g n) -> g n", n=GROUP))
+        load_scales(nc.scalar, tech_scale_raw[0], tech_scales, 0, 1)
+        load_words(tech_raw[0], tech_words, 0, 1)
+        load_words(duals[0], duals_words, 0, 1)
+        load_scales(nc.sync, duals_scale[0], duals_scales, 0, 2)
         load_shifts(0)
-        load_words(p_words[1], duals_words, G, 2 * G)
-        load_scales(ts_raw_rest, tech_scales, G, F)
-        load_words(t_raw_second, tech_words, G, 2 * G)
-        load_words(t_raw_rest, tech_words, 2 * G, F)
-        load_shifts(1)
-        load_shifts(2)
-        load_shifts(3)
-        load_scales(ps_last, duals_scales, 2 * G, C)
-        load_words(p_words[2], duals_words, 2 * G, C)
-        nc.sync.dma_start(out=weight_bf[:], in_=weight.rearrange("(c p j) -> p c j", p=P, j=4))
-        nc.sync.dma_start(out=alpha_bf[:], in_=alpha.rearrange("(c p j) -> p c j", p=P, j=4))
+        load_words(duals[1], duals_words, 1, 1)
+        load_scales(nc.sync, tech_scale_raw[1], tech_scales, 1, 3)
+        load_words(tech_raw[1], tech_words, 1, 1)
+        load_words(tech_raw[2], tech_words, 2, 2)
+        for g in range(1, VAR_GROUPS):
+            load_shifts(g)
+        load_scales(nc.sync, duals_scale[1], duals_scales, 2, 1)
+        load_words(duals[2], duals_words, 2, 1)
+        nc.sync.dma_start(out=weight_bf[:], in_=weight.rearrange("(c p j) -> p c j", p=P, j=PACK))
+        nc.sync.dma_start(out=alpha_bf[:], in_=alpha.rearrange("(c p j) -> p c j", p=P, j=PACK))
 
         nc.vector.tensor_copy(
-            out=cost_sorted[0:FG, :, :].rearrange("g t (u e) -> g t u e", e=4),
-            in_=cost_row[:].rearrange("g (u t e) -> g t u e", t=4, e=4),
+            out=cost_sorted[0:VAR_GROUPS, :, :].rearrange("g t (u e) -> g t u e", e=4),
+            in_=cost_rows[:].rearrange("g (u t e) -> g t u e", t=PACK, e=4),
         )
-        cost_bank = psum.tile([P, 4, P], BF16, name="bank")
-        for t in range(4):
-            nc.tensor.transpose(cost_bank[:, t, :], cost_sorted[:, t, :], ident[:])
-        nc.scalar.activation(out=cost_col[:], in_=cost_bank[:, :, 0:FG], func=IDENT)
-        nc.gpsimd.tensor_copy(out=weight_col[:], in_=weight_bf[:])
-        nc.gpsimd.tensor_tensor(out=offset_col[:], in0=weight_bf[:], in1=alpha_bf[:], op=MULT)
+        cost_bank = psum.tile([P, PACK, P], BF16, name="bank")
+        for t in range(PACK):
+            nc.tensor.transpose(cost_bank[:, t, :], cost_sorted[:, t, :], identity[:])
+        nc.scalar.activation(out=cost_col[:], in_=cost_bank[:, :, 0:VAR_GROUPS], func=IDENTITY)
 
-        sort_tech(0)
+        sort_tech_scales(0)
+        sort_tech_words(0)
         slopes(0, 0)
-        s_i(0)
-        s_q(0)
-        sort_tech(1)
+        interleave_shifts(0)
+        quantise_shifts(0)
+        sort_tech_scales(1)
+        sort_tech_words(1)
         slopes(1, 0)
-        d_i(0, 0)
-        sort_tech(2)
-        d_q(0, 0)
-        sort_tech(3)
+        interleave_slopes(0, 0)
+        sort_tech_words(2)
         slopes(0, 1)
-        s_i(1)
-        d_i(0, 1)
-        s_q(1)
+        interleave_slopes_shared(1, 0)
+        interleave_shifts(1)
+        interleave_slopes(0, 1)
         slopes(1, 1)
-        s_i(2)
-        d_q(0, 1)
-        s_i(3)
-        s_q(2)
+        interleave_shifts(2, 3)
+        quantise_shifts(1)
+        interleave_slopes(1, 1)
+        quantise_shifts(2, 3)
+        quantise_slopes(0, 0, 1)
         slopes(0, 2)
-        d_i(0, 2)
-        s_q(3)
         slopes(0, 3)
-        d_i(0, 3)
-        d_q(0, 2)
-        d_i(1, 0)
-        d_q(0, 3)
+        interleave_slopes(0, 2, 3)
+        quantise_slopes(1, 0, 1)
+        quantise_slopes(0, 2, 3)
         slopes(1, 2)
-        d_i(1, 1)
-        d_q(1, 0)
-        d_i(1, 2)
-        d_q(1, 1)
         slopes(1, 3)
-        d_i(1, 3)
-        d_q(1, 2)
+        nc.scalar.activation(out=weight_col[:], in_=weight_bf[:], func=IDENTITY)
+        nc.vector.tensor_tensor(out=offset_col[:], in0=weight_bf[:], in1=alpha_bf[:], op=mybir.AluOpType.mult)
+        interleave_slopes(1, 2, 3)
         slopes(2, 0)
-        d_i(2, 0)
-        d_q(1, 3)
+        interleave_slopes(2, 0)
+        quantise_slopes(1, 2, 3)
         slopes(2, 1)
-        d_i(2, 1)
-        d_q(2, 0)
-        for j in range(4):
-            values(0, j)
-        store_y(0)
-        y_i(0)
-        d_q(2, 1)
+        interleave_slopes(2, 1)
+        quantise_slopes(2, 0)
+        values(0)
+        interleave_y(0)
+        quantise_slopes(2, 1)
         slopes(2, 2)
-        d_i(2, 2)
-        y_q(0)
-        store_codes(0, 0, 512)
+        interleave_slopes(2, 2)
+        quantise_y(0)
+        store_codes(0, 0, PLANS)
         slopes(2, 3)
-        d_i(2, 3)
-        d_q(2, 2)
-        d_q(2, 3)
-        for j in range(4):
-            values(1, j)
-        store_y(1)
-        y_i(1)
-        for j in range(4):
-            values(2, j)
-        store_y(2)
-        y_i(2)
-        y_q(1)
-        y_q(2)
-        store_codes(1, 0, 512)
+        interleave_slopes(2, 3)
+        quantise_slopes(2, 2)
+        quantise_slopes(2, 3)
+
+        values(1)
+        interleave_y(1)
+        values(2)
+        interleave_y(2)
+        quantise_y(1)
+        quantise_y(2)
+        store_codes(1, 0, PLANS)
         store_scales(0, 2, [nc.sync] * 4)
-        for j in range(4):
-            values(3, j)
-        store_y(3)
-        y_i(3)
-        y_q(3)
-        store_codes(2, 0, 256)
-        for j in range(4):
-            values(4, j)
-        store_y(4)
-        y_i(4)
-        for j in range(4):
-            values(5, j)
-        store_y(5)
-        y_i(5)
-        y_q(4)
-        y_q(5)
-        store_codes(2, 256, 512)
+        values(3)
+        interleave_y(3)
+        quantise_y(3)
+        store_codes(2, 0, PIECES[4][1])
+        values(4)
+        interleave_y(4)
+        values(5)
+        interleave_y(5)
+        quantise_y(4)
+        quantise_y(5)
+        store_codes(2, PIECES[4][1], PLANS)
         store_scales(2, 3, [nc.scalar, nc.sync, nc.scalar, nc.sync])

from contextlib import ExitStack

import concourse.mybir as mybir
from concourse.masks import make_identity

CUTS, CONSTRAINTS, VARIABLES, PLANS = 1536, 1024, 2048, 512
FLOPS = 2 * CONSTRAINTS * CUTS * VARIABLES + 2 * CUTS * VARIABLES * PLANS

F32 = mybir.dt.float32
BF16 = mybir.dt.bfloat16
I32 = mybir.dt.int32
U32 = mybir.dt.uint32
U8 = mybir.dt.uint8
FP8X4 = mybir.dt.float8_e4m3fn_x4
FP4X4 = mybir.dt.float4_e2m1fn_x4
IDENTITY = mybir.ActivationFunctionType.Identity

P = 128
PACK = 4
GROUP = P * PACK
K_GROUPS = CONSTRAINTS // GROUP
VAR_GROUPS = VARIABLES // GROUP
CUT_GROUPS = CUTS // GROUP
FP4_BYTES = 2
QUADRANT = 32
RUN = 4

SHIFT_SETS = [(0,), (1,), (2, 3)]
SLOPE_SETS = [(c, gs) for c in (0, 1) for gs in ((0, 1), (2, 3))] + [(2, (g,)) for g in range(VAR_GROUPS)]

PIECES = [(0, 0, 512), (1, 0, 256), (1, 256, 256), (2, 0, 256), (2, 256, 128), (2, 384, 128)]

SINGLE_BUFS, PAIR_BUFS = 4, 3


def tile_benders_cut_values_k5_kernel(
    tc, duals_words, duals_scales, tech_words, tech_scales, cost, shifts, alpha, weight, out_0, out_1, out_2
):
    nc = tc.nc
    with ExitStack() as ctx:
        keep = ctx.enter_context(tc.tile_pool(name="keep", bufs=1))
        stage = ctx.enter_context(tc.tile_pool(name="stage", bufs=SINGLE_BUFS))
        psum = ctx.enter_context(tc.psum_pool(name="psum", bufs=8))
        ctx.enter_context(tc.manual_schedule())

        def kept(name, shape, dtype):
            return keep.tile(shape, dtype, name=name, align_bytes=256)

        tech_raw = [kept("tech_raw%d" % n, [P, K_GROUPS, w * FP4_BYTES * GROUP], U8) for n, w in enumerate((1, 1, 2))]
        tech_scale_raw = [kept("tech_scale_raw%d" % n, [P, K_GROUPS, w * GROUP], U8) for n, w in enumerate((1, 3))]
        tech_sorted = [
            kept("tech_sorted%d" % n, [P, K_GROUPS, w * FP4_BYTES * GROUP], U8) for n, w in enumerate((1, 1, 2))
        ]
        tech_scale_sorted = [
            kept("tech_scale_sorted%d" % n, [P, K_GROUPS, w * GROUP], U8) for n, w in enumerate((1, 3))
        ]
        tech_of_group = tech_sorted[:2] + [
            tech_sorted[2][:, :, h * FP4_BYTES * GROUP : (h + 1) * FP4_BYTES * GROUP] for h in range(2)
        ]
        tech_scale_of_group = tech_scale_sorted[:1] + [
            tech_scale_sorted[1][:, :, h * GROUP : (h + 1) * GROUP] for h in range(3)
        ]
        duals = [kept("duals%d" % c, [P, K_GROUPS, FP4_BYTES * GROUP], U8) for c in range(CUT_GROUPS)]
        duals_scale = [kept("duals_scale%d" % n, [P, K_GROUPS, w * GROUP], U8) for n, w in enumerate((2, 1))]
        duals_scale_of_group = [duals_scale[0][:, :, h * GROUP : (h + 1) * GROUP] for h in range(2)] + duals_scale[1:]

        shift_rows, shift_codes, shift_scales = {}, {}, {}
        for gs in SHIFT_SETS:
            shift_rows[gs] = kept("shift_rows%d" % gs[0], [P, PACK, len(gs), PLANS], BF16)
            shift_codes[gs] = kept("shift_codes%d" % gs[0], [P, len(gs) * PLANS], U32)
            shift_scales[gs] = kept("shift_scales%d" % gs[0], [P, len(gs) * PLANS], U8)
        slope_rows, slope_codes, slope_scales = {}, {}, {}
        for c, gs in SLOPE_SETS:
            slope_rows[c, gs] = kept("slope_rows%d_%d" % (c, gs[0]), [P, PACK, len(gs), GROUP], BF16)
            slope_codes[c, gs] = kept("slope_codes%d_%d" % (c, gs[0]), [P, len(gs) * GROUP], U32)
            slope_scales[c, gs] = kept("slope_scales%d_%d" % (c, gs[0]), [P, len(gs) * GROUP], U8)
        shift_set_of = {g: gs for gs in SHIFT_SETS for g in gs}
        slope_set_of = {(c, g): gs for c, gs in SLOPE_SETS for g in gs}

        cost_rows = kept("cost_rows", [VAR_GROUPS, GROUP], BF16)
        cost_sorted = kept("cost_sorted", [P, PACK, P], BF16)
        cost_col = kept("cost_col", [P, PACK, VAR_GROUPS], F32)
        identity = kept("identity", [P, P], BF16)
        alpha_bf = kept("alpha_bf", [P, CUT_GROUPS, PACK], BF16)
        weight_bf = kept("weight_bf", [P, CUT_GROUPS, PACK], BF16)
        weight_col = kept("weight_col", [P, CUT_GROUPS, PACK], F32)
        offset_col = kept("offset_col", [P, CUT_GROUPS, PACK], F32)
        y = [kept("y%d" % n, [P, PACK, width], F32) for n, (c, first, width) in enumerate(PIECES)]
        y_codes = kept("y_codes", [P, CUT_GROUPS, PLANS], U32)
        y_scales = kept("y_scales", [P, CUT_GROUPS, PLANS], U8)

        def flat_words(tile):
            return tile[:].rearrange("p k n -> p (k n)").bitcast(I32)


        def load_words(tile, src, first_group, groups):
            cols = slice(FP4_BYTES * GROUP * first_group, FP4_BYTES * GROUP * (first_group + groups))
            nc.sync.dma_start(out=tile[:].bitcast(I32), in_=src.rearrange("k p n -> p k n")[:, :, cols].bitcast(I32))

        def load_scales(queue, tile, src, first_group, groups):
            cols = slice(GROUP * first_group, GROUP * (first_group + groups))
            for r in range(4):
                queue.dma_start(
                    out=tile[r:P:QUADRANT, :, :].bitcast(I32),
                    in_=src.rearrange("k (q r) n -> r q k n", r=4)[r, :, :, cols].bitcast(I32),
                )

        def load_shifts(g):
            gs = shift_set_of[g]
            rows = shifts[g * GROUP : (g + 1) * GROUP, :].rearrange("(u t e) m -> e u t m", t=PACK, e=4)
            for e in range(4):
                nc.sync.dma_start(out=shift_rows[gs][e:P:4, :, gs.index(g), :], in_=rows[e])


        def sort_tech_scales(n):
            nc.vector.tensor_copy(
                out=flat_words(tech_scale_sorted[n]).rearrange("p (a t u) -> p a t u", t=PACK, u=32),
                in_=flat_words(tech_scale_raw[n]).rearrange("p (a u t) -> p a t u", t=PACK, u=32),
            )

        def sort_tech_words(n):
            nc.vector.tensor_copy(
                out=flat_words(tech_sorted[n]).rearrange("p (a t u w) -> p a t u w", t=PACK, u=32, w=2),
                in_=flat_words(tech_raw[n]).rearrange("p (a u t w) -> p a t u w", t=PACK, u=32, w=2),
            )


        interleaved = {}

        def new_interleaved(key, shape, pair):
            name, bufs = ("interleaved_pair", PAIR_BUFS) if pair else ("interleaved", SINGLE_BUFS)
            interleaved[key] = stage.tile(shape, BF16, name=name, bufs=bufs, align_bytes=256)

        def interleave(key, rows, width):
            new_interleaved(key, [P, width, PACK], width > GROUP)
            nc.vector.tensor_copy(
                out=interleaved[key][:].rearrange("p (x i) t -> p x t i", i=RUN),
                in_=rows.rearrange("p t (x i) -> p x t i", i=RUN),
            )

        def quantise(key, codes, scales):
            nc.vector.quantize_mx(
                out=codes.bitcast(FP8X4), scales=scales, in_=interleaved[key][:].rearrange("p x t -> p (x t)")
            )

        def interleave_shifts(*gs):
            interleave(("shifts", gs), shift_rows[gs][:].rearrange("p t g m -> p t (g m)"), len(gs) * PLANS)

        def quantise_shifts(*gs):
            quantise(("shifts", gs), shift_codes[gs][:], shift_scales[gs][:])


        def slopes(c, g):
            gs = slope_set_of[c, g]
            for t in range(PACK):
                bank = psum.tile([P, GROUP], F32, name="bank")
                for k in range(K_GROUPS):
                    nc.tensor.matmul_mx(
                        out=bank[:],
                        lhsT=tech_of_group[g][:, k, FP4_BYTES * P * t : FP4_BYTES * P * (t + 1)].bitcast(FP4X4),
                        lhsT_scale=tech_scale_of_group[g][:, k, P * t : P * (t + 1)],
                        rhs=duals[c][:, k, :].bitcast(FP4X4),
                        rhs_scale=duals_scale_of_group[c][:, k, :],
                        start=(k == 0),
                        stop=(k == K_GROUPS - 1),
                    )
                nc.scalar.activation(
                    out=slope_rows[c, gs][:, t, gs.index(g), :].rearrange("p (h m b) -> p h m b", h=2, b=2),
                    in_=bank[:].rearrange("p (m h b) -> p h m b", h=2, b=2),
                    func=IDENTITY,
                    bias=cost_col[:, t, g : g + 1],
                    scale=-1.0,
                )

        def slope_views(c, part):
            gs = slope_set_of[c, part[0]]
            if ("slopes", c, gs) not in interleaved:
                new_interleaved(("slopes", c, gs), [P, 2, len(gs), GROUP // 2, PACK], len(gs) > 1)
            groups = slice(gs.index(part[0]), gs.index(part[0]) + len(part))
            dst = interleaved["slopes", c, gs][:, :, groups, :, :].rearrange("p b g (x i) t -> p (g x) b t i", i=RUN)
            src = slope_rows[c, gs][:, :, groups, :].rearrange("p t g (x i b) -> p (g x) b t i", b=2, i=RUN)
            return dst, src

        def interleave_slopes(c, *part):
            dst, src = slope_views(c, part)
            nc.vector.tensor_copy(out=dst, in_=src)

        def interleave_slopes_shared(c, g):
            dst, src = slope_views(c, (g,))
            nc.scalar.activation(out=dst[:, :, 0, :, :], in_=src[:, :, 0, :, :], func=IDENTITY)
            nc.vector.tensor_copy(out=dst[:, :, 1, :, :], in_=src[:, :, 1, :, :])

        def quantise_slopes(c, *gs):
            nc.vector.quantize_mx(
                out=slope_codes[c, gs][:].bitcast(FP8X4),
                scales=slope_scales[c, gs][:],
                in_=interleaved["slopes", c, gs][:].rearrange("p b g n t -> p (b g n t)"),
            )


        def values(n):
            c, first, width = PIECES[n]
            for j in range(PACK):
                bank = psum.tile([P, width], F32, name="bank")
                for g in range(VAR_GROUPS):
                    slope_set, shift_set = slope_set_of[c, g], shift_set_of[g]
                    cut_col = P * (2 * len(slope_set) * (j % 2) + 2 * slope_set.index(g) + j // 2)
                    plan_col = shift_set.index(g) * PLANS + first
                    nc.tensor.matmul_mx(
                        out=bank[:],
                        lhsT=slope_codes[c, slope_set][:, cut_col : cut_col + P].bitcast(FP8X4),
                        lhsT_scale=slope_scales[c, slope_set][:, cut_col : cut_col + P],
                        rhs=shift_codes[shift_set][:, plan_col : plan_col + width].bitcast(FP8X4),
                        rhs_scale=shift_scales[shift_set][:, plan_col : plan_col + width],
                        start=(g == 0),
                        stop=(g == VAR_GROUPS - 1),
                    )
                nc.scalar.activation(
                    out=y[n][:, j, :],
                    in_=bank[:],
                    func=IDENTITY,
                    bias=offset_col[:, c, j : j + 1],
                    scale=weight_col[:, c, j : j + 1],
                )
            nc.sync.dma_start(
                out=out_0[c * GROUP : (c + 1) * GROUP, first : first + width].rearrange("(p j) m -> p j m", j=PACK),
                in_=y[n][:],
            )

        def interleave_y(n):
            interleave(("y", n), y[n][:], PIECES[n][2])

        def quantise_y(n):
            c, first, width = PIECES[n]
            quantise(("y", n), y_codes[:, c, first : first + width], y_scales[:, c, first : first + width])

        def store_codes(c, first, end):
            nc.sync.dma_start(
                out=out_1[c].rearrange("p m t -> p (m t)")[:, PACK * first : PACK * end].bitcast(I32),
                in_=y_codes[:, c, first:end].bitcast(I32),
            )

        def store_scales(first_group, end_group, queues):
            for r in range(4):
                queues[r].dma_start(
                    out=out_2.rearrange("c (q r) m -> r q c m", r=4)[r, :, first_group:end_group, :].bitcast(I32),
                    in_=y_scales[r:P:QUADRANT, first_group:end_group, :].bitcast(I32),
                )

        nc.vector.memset(flat_words(tech_scale_raw[0]), 0)
        nc.vector.memset(flat_words(duals_scale[0]), 0)
        nc.vector.memset(cost_sorted[:], 0.0)
        nc.vector.memset(flat_words(tech_scale_raw[1]), 0)
        nc.vector.memset(flat_words(duals_scale[1]), 0)
        make_identity(nc, identity[:])

        nc.sync.dma_start(out=cost_rows[:], in_=cost.rearrange("(g n) -> g n", n=GROUP))
        load_scales(nc.scalar, tech_scale_raw[0], tech_scales, 0, 1)
        load_words(tech_raw[0], tech_words, 0, 1)
        load_words(duals[0], duals_words, 0, 1)
        load_scales(nc.sync, duals_scale[0], duals_scales, 0, 2)
        load_shifts(0)
        load_words(duals[1], duals_words, 1, 1)
        load_scales(nc.sync, tech_scale_raw[1], tech_scales, 1, 3)
        load_words(tech_raw[1], tech_words, 1, 1)
        load_words(tech_raw[2], tech_words, 2, 2)
        for g in range(1, VAR_GROUPS):
            load_shifts(g)
        load_scales(nc.sync, duals_scale[1], duals_scales, 2, 1)
        load_words(duals[2], duals_words, 2, 1)
        nc.sync.dma_start(out=weight_bf[:], in_=weight.rearrange("(c p j) -> p c j", p=P, j=PACK))
        nc.sync.dma_start(out=alpha_bf[:], in_=alpha.rearrange("(c p j) -> p c j", p=P, j=PACK))

        nc.vector.tensor_copy(
            out=cost_sorted[0:VAR_GROUPS, :, :].rearrange("g t (u e) -> g t u e", e=4),
            in_=cost_rows[:].rearrange("g (u t e) -> g t u e", t=PACK, e=4),
        )
        cost_bank = psum.tile([P, PACK, P], BF16, name="bank")
        for t in range(PACK):
            nc.tensor.transpose(cost_bank[:, t, :], cost_sorted[:, t, :], identity[:])
        nc.scalar.activation(out=cost_col[:], in_=cost_bank[:, :, 0:VAR_GROUPS], func=IDENTITY)

        sort_tech_scales(0)
        sort_tech_words(0)
        slopes(0, 0)
        interleave_shifts(0)
        quantise_shifts(0)
        sort_tech_scales(1)
        sort_tech_words(1)
        slopes(1, 0)
        interleave_slopes(0, 0)
        sort_tech_words(2)
        slopes(0, 1)
        interleave_slopes_shared(1, 0)
        interleave_shifts(1)
        interleave_slopes(0, 1)
        slopes(1, 1)
        interleave_shifts(2, 3)
        quantise_shifts(1)
        interleave_slopes(1, 1)
        quantise_shifts(2, 3)
        quantise_slopes(0, 0, 1)
        slopes(0, 2)
        slopes(0, 3)
        interleave_slopes(0, 2, 3)
        quantise_slopes(1, 0, 1)
        quantise_slopes(0, 2, 3)
        slopes(1, 2)
        slopes(1, 3)
        nc.scalar.activation(out=weight_col[:], in_=weight_bf[:], func=IDENTITY)
        nc.vector.tensor_tensor(out=offset_col[:], in0=weight_bf[:], in1=alpha_bf[:], op=mybir.AluOpType.mult)
        interleave_slopes(1, 2, 3)
        slopes(2, 0)
        interleave_slopes(2, 0)
        quantise_slopes(1, 2, 3)
        slopes(2, 1)
        interleave_slopes(2, 1)
        quantise_slopes(2, 0)
        values(0)
        interleave_y(0)
        quantise_slopes(2, 1)
        slopes(2, 2)
        interleave_slopes(2, 2)
        quantise_y(0)
        store_codes(0, 0, PLANS)
        slopes(2, 3)
        interleave_slopes(2, 3)
        quantise_slopes(2, 2)
        quantise_slopes(2, 3)

        values(1)
        interleave_y(1)
        values(2)
        interleave_y(2)
        quantise_y(1)
        quantise_y(2)
        store_codes(1, 0, PLANS)
        store_scales(0, 2, [nc.sync] * 4)
        values(3)
        interleave_y(3)
        quantise_y(3)
        store_codes(2, 0, PIECES[4][1])
        values(4)
        interleave_y(4)
        values(5)
        interleave_y(5)
        quantise_y(4)
        quantise_y(5)
        store_codes(2, PIECES[4][1], PLANS)
        store_scales(2, 3, [nc.scalar, nc.sync, nc.scalar, nc.sync])
